import numpy as np
import ml_dtypes


def mxq(x, axis, fmt="e4m3"):
    dtype, down = {"e4m3": (ml_dtypes.float8_e4m3fn, 7), "e5m2": (ml_dtypes.float8_e5m2, 14)}[fmt]
    v = np.moveaxis(np.asarray(x, np.float32).astype(ml_dtypes.bfloat16).astype(np.float64), axis, -1)
    blocks = v.reshape(v.shape[:-1] + (-1, 32))
    amax = np.abs(blocks).max(-1, keepdims=True)
    byte = np.maximum(np.where(amax > 0, np.frexp(amax)[1] - 1 + 127, 0) - down, 1)
    scale = np.exp2(byte - 127.0)
    codes = (blocks / scale).astype(np.float32).astype(dtype).astype(np.float64)
    return np.moveaxis((codes * scale).reshape(v.shape), -1, axis)


WIDE = False


def mx_kscale(k):
    if not WIDE:
        return np.ones(k)
    levels = np.array([10, -10, 5, -5, 0])
    if k % 512:
        return np.exp2(np.random.permutation(np.resize(levels, k // 32))).repeat(32)
    a = np.empty((k // 512, 16))
    for p in range(k // 512):
        a[p, :8] = np.random.permutation(np.resize(levels, 8))
        for g in range(8):
            far = levels[np.abs(levels - a[p, g]) >= 10]
            a[p, g + 8] = far[np.random.randint(len(far))]
    return np.exp2(a.ravel()).repeat(32)


def f64(x):
    return np.asarray(x).astype(np.float64)


def striped(idx):
    return np.tile(idx.reshape(-1, 16).T, (8, 1)).astype(np.uint16)


def unstriped(offs):
    return offs[:16].T.reshape(-1).astype(np.int64)


def pack_weight(w):
    k, n = w.shape
    w = f64(np.asarray(w, np.float32).astype(ml_dtypes.bfloat16)).reshape(k // 32, 32, n)
    amax = np.abs(w).max(1)
    byte = np.clip(np.where(amax > 0, np.frexp(amax)[1] - 1 + 127 - 7, 1), 1, 254)
    scaled = (w * np.exp2(127.0 - byte)[:, None, :]).reshape(k, n).astype(np.float32)
    words = np.ascontiguousarray(scaled.reshape(k // 512, 128, 4, n).transpose(0, 1, 3, 2)).astype(ml_dtypes.float8_e4m3fn).view(np.uint8)
    return words, np.ascontiguousarray(byte.astype(np.uint8).reshape(k // 512, 16, n))


def unpack_weight(words, scales):
    g, p, n, _ = words.shape
    vals = np.ascontiguousarray(words).view(ml_dtypes.float8_e4m3fn).astype(np.float64) * np.repeat(np.exp2(scales.astype(np.float64) - 127.0), 8, axis=1)[..., None]
    return vals.transpose(0, 1, 3, 2).reshape(g * 512, n)


E2M1 = np.array([0.0, 0.5, 1.0, 1.5, 2.0, 3.0, 4.0, 6.0, -0.0, -0.5, -1.0, -1.5, -2.0, -3.0, -4.0, -6.0])


def pack_fp4(w):
    k, n = w.shape
    w = f64(np.asarray(w, np.float32).astype(ml_dtypes.bfloat16)).reshape(k // 32, 32, n)
    amax = np.abs(w).max(1)
    mant, ex = np.frexp(amax / 6.0)
    byte = np.clip(np.where(amax > 0, np.where(mant > 0.5, ex, ex - 1) + 127, 1), 1, 254)
    scaled = (w * np.exp2(127.0 - byte)[:, None, :]).reshape(k, n).astype(np.float32)
    c = np.ascontiguousarray(scaled.reshape(k // 512, 128, 4, n).transpose(0, 1, 3, 2)).astype(ml_dtypes.float4_e2m1fn).view(np.uint8) & 0xF
    words = (c[..., 0::2] | (c[..., 1::2] << 4)).reshape(k // 512, 128, 2 * n)
    return np.ascontiguousarray(words), np.ascontiguousarray(byte.astype(np.uint8).reshape(k // 512, 16, n))


def unpack_fp4(words, scales):
    g, _, n = scales.shape
    words = np.ascontiguousarray(words).reshape(g, 128, n, 2)
    nib = np.empty((g, 128, n, 4), np.uint8)
    nib[..., 0::2] = words & 0xF
    nib[..., 1::2] = words >> 4
    vals = E2M1[nib] * np.repeat(np.exp2(scales.astype(np.float64) - 127.0), 8, axis=1)[..., None]
    return vals.transpose(0, 1, 3, 2).reshape(g * 512, n)


def sigmoid(v):
    return 1.0 / (1.0 + np.exp(-np.maximum(v, -700.0)))


K, T, S, N, H, U = 512, 2048, 512, 256, 512, 1024


def setup_inputs():
    n = np.random.standard_normal
    s = mx_kscale(K)[:, None]
    u = mx_kscale(H)
    packed_xT = pack_weight(n((K, T)) * s)
    packed_w1 = pack_fp4(n((K, H)) / np.sqrt(K) / s)
    packed_w2 = pack_fp4(n((K, H)) / np.sqrt(K) / s)
    packed_w3 = pack_fp4(n((H, N)) / np.sqrt(H) / u[:, None])
    return {
        "x_words": packed_xT[0],
        "x_scales": packed_xT[1],
        "w1_words": packed_w1[0],
        "w1_scales": packed_w1[1],
        "w2_words": packed_w2[0],
        "w2_scales": packed_w2[1],
        "nl": (np.random.uniform(0.1, 1.0, (H, U))).astype(np.float32),
        "lh": (np.random.uniform(0.1, 1.0, (H, U))).astype(np.float32),
        "unit": (np.random.uniform(0.6, 1.4, (H, 1)) * u[:, None]).astype(np.float32),
        "w3_words": packed_w3[0],
        "w3_scales": packed_w3[1],
        "offs": striped(np.random.permutation(T)[:S]),
        "mat": striped(np.random.permutation(np.concatenate([np.arange(S), np.random.randint(0, S, U - S)]))),
        "tint": striped(np.random.permutation(np.concatenate([np.arange(S), np.random.randint(0, S, U - S)]))),
    }


def reference(x_words, x_scales, w1_words, w1_scales, w2_words, w2_scales, nl, lh, unit, w3_words, w3_scales, offs, mat, tint):
    xq = unpack_weight(x_words, x_scales)[:, unstriped(offs)]
    bc = unpack_fp4(w1_words, w1_scales).T @ xq
    bm = bc[:, unstriped(mat)]
    rg = unpack_fp4(w2_words, w2_scales).T @ xq
    alph = 0.7 * sigmoid(rg) + 0.2
    am = alph[:, unstriped(mat)]
    fd = 2.0 * (am * ((f64(lh)) ** 2)) - 0.5
    fsh = ((-1.0 * f64(nl) + 1.0) ** 2) / (f64(nl) + 0.3)
    diff = bm * (fd * fsh + 1.0)
    bt = bc[:, unstriped(tint)]
    sheen = bt * fsh
    hid = f64(unit) * (diff * (-1.0 * (0.6 * sigmoid(sheen)) + 1.0))
    return unpack_fp4(w3_words, w3_scales).T @ mxq(hid, 0, "e4m3")

@@ -1,0 +1,305 @@
+from contextlib import ExitStack
+
+import concourse.mybir as mybir
+from concourse.masks import make_identity
+
+F32 = mybir.dt.float32
+BF16 = mybir.dt.bfloat16
+I32 = mybir.dt.int32
+U32 = mybir.dt.uint32
+U16 = mybir.dt.uint16
+U8 = mybir.dt.uint8
+FP8X4 = mybir.dt.float8_e4m3fn_x4
+FP4X4 = mybir.dt.float4_e2m1fn_x4
+ACT = mybir.ActivationFunctionType
+ALU = mybir.AluOpType
+
+P = 128
+K, T, S, N, H, U = 512, 2048, 512, 256, 512, 1024
+PACK = 4
+BANK = 512
+WINDOW = S + 32
+CHUNKS = (512, 256, 256)
+FLOPS = 2 * (2 * K * H * S + H * N * U)
+
+
+def load_scale_rows(queue, plane, rows):
+    for q in range(4):
+        queue.dma_start(out=plane[32 * q : 32 * q + 4, :].bitcast(I32), in_=rows[4 * q : 4 * q + 4, :].bitcast(I32))
+
+
+def tile_picked_ydisny_weak_p_kernel(
+    tc, x_words, x_scales, w1_words, w1_scales, w2_words, w2_scales, nl, lh, unit, w3_words, w3_scales, offs, mat, tint, out
+):
+    nc = tc.nc
+    with ExitStack() as ctx:
+        keep = ctx.enter_context(tc.tile_pool(name="keep", bufs=1))
+        ring2 = ctx.enter_context(tc.tile_pool(name="ring2", bufs=2))
+        ring3 = ctx.enter_context(tc.tile_pool(name="ring3", bufs=3))
+        psum_t = ctx.enter_context(tc.psum_pool(name="psum_t", bufs=3))
+        psum_f = ctx.enter_context(tc.psum_pool(name="psum_f", bufs=3))
+        psum_mm = ctx.enter_context(tc.psum_pool(name="psum_mm", bufs=2))
+
+        offs_sb = keep.tile([P, S // 16], U16, name="offs_sb")
+        mat_sb = keep.tile([P, U // 16], U16, name="mat_sb")
+        tint_sb = keep.tile([P, U // 16], U16, name="tint_sb")
+        x_table = keep.tile([P, T], I32, name="x_table", align_bytes=64)
+        x_plane = keep.tile([P, T], U8, name="x_plane", align_bytes=64)
+        w_raw = [keep.tile([P, 2 * H], U8, name="w_raw%d" % i, align_bytes=64) for i in range(2)]
+        w_plane_raw = [keep.tile([P, H], U8, name="w_plane_raw%d" % i, align_bytes=64) for i in range(2)]
+        w3_sb = keep.tile([P, 2 * N], U8, name="w3_sb", align_bytes=64)
+        w3_plane = keep.tile([P, N], U8, name="w3_plane", align_bytes=64)
+        unit_sb = keep.tile([P, PACK], F32, name="unit_sb")
+        ident = keep.tile([P, P], F32, name="ident")
+        bc_win = [keep.tile([P, WINDOW], F32, name="bc_win%d" % t) for t in range(PACK)]
+        rough_win = [keep.tile([P, WINDOW], F32, name="rough_win%d" % t) for t in range(PACK)]
+
+        make_identity(nc, ident[:])
+        nc.vector.memset(x_plane[:].bitcast(I32), 0)
+        for plane in w_plane_raw + [w3_plane]:
+            nc.vector.memset(plane[:].bitcast(I32), 0)
+        for win in bc_win + rough_win:
+            nc.vector.memset(win[:, S:WINDOW], 0.0)
+
+        nl_rows = nl.rearrange("(p t) r -> p t r", t=PACK)
+        lh_rows = lh.rearrange("(p t) r -> p t r", t=PACK)
+        nl_sb, lh_sb = {}, {}
+
+        def load_rows(held, rows, label, half, t0, t1):
+            piece = keep.tile([P, t1 - t0, BANK], F32, name="%s_%d_%d" % (label, half, t0))
+            nc.sync.dma_start(out=piece[:], in_=rows[:, t0:t1, half * BANK : (half + 1) * BANK])
+            for t in range(t0, t1):
+                held[half, t] = piece[:, t - t0, :]
+
+        def load_words(tile, words):
+            nc.sync.dma_start(out=tile[:].bitcast(I32), in_=words.bitcast(I32))
+
+        load_rows(nl_sb, nl_rows, "nl", 0, 0, 1)
+        load_words(w_raw[0], w1_words[0])
+        load_words(w_raw[1], w2_words[0])
+        load_rows(nl_sb, nl_rows, "nl", 0, 1, 2)
+        load_rows(nl_sb, nl_rows, "nl", 0, 2, 4)
+        load_scale_rows(nc.sync, w_plane_raw[0], w1_scales[0])
+        load_rows(lh_sb, lh_rows, "lh", 0, 0, 2)
+        load_scale_rows(nc.sync, w_plane_raw[1], w2_scales[0])
+        load_rows(nl_sb, nl_rows, "nl", 1, 0, 2)
+        nc.sync.dma_start(offs_sb[:], offs)
+        load_scale_rows(nc.sync, x_plane, x_scales[0])
+        load_rows(lh_sb, lh_rows, "lh", 0, 2, 4)
+        load_rows(nl_sb, nl_rows, "nl", 1, 2, 4)
+        nc.sync.dma_start(out=x_table[:], in_=x_words[0].rearrange("p c j -> p (c j)").bitcast(I32))
+        load_rows(lh_sb, lh_rows, "lh", 1, 0, 2)
+        nc.sync.dma_start(out=unit_sb[:], in_=unit.rearrange("(p t) o -> p (t o)", t=PACK))
+        nc.sync.dma_start(tint_sb[:], tint)
+        nc.sync.dma_start(mat_sb[:], mat)
+        load_rows(lh_sb, lh_rows, "lh", 1, 2, 4)
+        load_words(w3_sb, w3_words[0])
+        load_scale_rows(nc.sync, w3_plane, w3_scales[0])
+
+        coef = keep.tile([P, 4, PACK], F32, name="coef")
+        for row, factor in enumerate((-0.6 * 1.4, -0.6 * 0.4, 0.6 * 0.5, -0.6)):
+            nc.vector.tensor_scalar(coef[:, row, :], unit_sb[:], factor, 0.0, ALU.mult, ALU.add)
+
+        plus, rest, lh_sq = {}, {}, {}
+
+        def fsh_terms(half, t):
+            nl_t = psum_t.tile([P, BANK], F32, name="turned")
+            for b in range(BANK // P):
+                nc.tensor.transpose(nl_t[:, b * P : (b + 1) * P], nl_sb[half, t][:, b * P : (b + 1) * P], ident[:])
+            root = ring2.tile([P, BANK], F32, name="root")
+            nc.scalar.activation(root[:], nl_t[:], ACT.Abs_reciprocal_sqrt, bias=0.3 / 1.69, scale=1.0 / 1.69)
+            inv = ring3.tile([P, BANK], F32, name="inv")
+            nc.scalar.activation(inv[:], root[:], ACT.Square)
+            plus[half, t] = keep.tile([P, BANK], F32, name="plus_%d_%d" % (half, t))
+            rest[half, t] = keep.tile([P, BANK], F32, name="rest_%d_%d" % (half, t))
+            nc.vector.scalar_tensor_tensor(plus[half, t][:], nl_t[:], -0.3, inv[:], ALU.is_gt, ALU.mult)
+            nc.vector.scalar_tensor_tensor(rest[half, t][:], nl_t[:], -2.3, inv[:], ALU.add, ALU.subtract)
+
+        def square_lh(half, t):
+            lh_sq[half, t] = keep.tile([P, BANK], F32, name="lh_sq_%d_%d" % (half, t))
+            if (half, t) in ():
+                nc.scalar.activation(lh_sq[half, t][:], lh_sb[half, t], ACT.Square)
+            else:
+                nc.gpsimd.tensor_tensor(lh_sq[half, t][:], lh_sb[half, t], lh_sb[half, t], ALU.mult)
+
+        xq_words = keep.tile([P, S], U32, name="xq_words", align_bytes=64)
+        xq_plane = keep.tile([P, S], U8, name="xq_plane", align_bytes=64)
+        w_dealt = [keep.tile([P, PACK, 2 * P], U8, name="w_dealt%d" % i, align_bytes=64) for i in range(2)]
+        w_plane = [keep.tile([P, PACK, P], U8, name="w_plane%d" % i, align_bytes=64) for i in range(2)]
+
+        def deal_words(i):
+            nc.vector.tensor_copy(
+                w_dealt[i][:].rearrange("p t (m e) -> p t m e", e=2),
+                w_raw[i][:].rearrange("p (m t e) -> p t m e", t=PACK, e=2),
+            )
+
+        def deal_scales(i):
+            nc.gpsimd.tensor_copy(w_plane[i][:], w_plane_raw[i][:].rearrange("p (m t) -> p t m", t=PACK))
+
+        def first_product(i, t, pool, label):
+            acc = pool.tile([P, S], F32, name=label)
+            nc.tensor.matmul_mx(
+                out=acc[:],
+                lhsT=w_dealt[i][:, t, :].bitcast(FP4X4),
+                lhsT_scale=w_plane[i][:, t, :],
+                rhs=xq_words[:].bitcast(FP8X4),
+                rhs_scale=xq_plane[:],
+                start=True,
+                stop=True,
+            )
+            return acc
+
+        def colour_window(t):
+            acc = first_product(0, t, psum_mm, "acc")
+            nc.scalar.copy(bc_win[t][:, :S], acc[:])
+
+        def rough_window(t):
+            acc = first_product(1, t, psum_t, "turned")
+            sig = ring2.tile([P, S], F32, name="sig")
+            nc.scalar.activation(sig[:], acc[:], ACT.Sigmoid)
+            nc.vector.tensor_scalar(
+                rough_win[t][:, :S], sig[:], coef[:, 0, t : t + 1], coef[:, 1, t : t + 1], ALU.mult, ALU.add
+            )
+
+        units = [(half, t) for half in range(U // BANK) for t in range(PACK)]
+        deal_words(0)
+        deal_words(1)
+        for index, (half, t) in enumerate(units):
+            fsh_terms(half, t)
+            square_lh(half, t)
+            if index == 1:
+                deal_scales(0)
+                deal_scales(1)
+            if index == 4:
+                nc.vector.tensor_copy(xq_plane[:], x_plane[:].indirect(offs_sb[:]))
+            if index == 6:
+                nc.vector.tensor_copy(xq_words[:], x_table[:].bitcast(U32).indirect(offs_sb[:]))
+
+        steps = []
+        start = 0
+        for width in CHUNKS:
+            steps.extend([(start, width, t) for t in range(PACK)])
+            start = start + width
+        state = {}
+
+        def fetch(step):
+            c0, width, t = step
+            lists = slice(c0 // 16, (c0 + width) // 16)
+            half, inner = divmod(c0, BANK)
+            bt = ring3.tile([P, width], F32, name="bt")
+            nc.scalar.activation(bt[:], bc_win[t][:].indirect(tint_sb[:, lists]), ACT.Copy)
+            bm = ring3.tile([P, width], F32, name="bm")
+            nc.scalar.activation(bm[:], bc_win[t][:].indirect(mat_sb[:, lists]), ACT.Copy)
+            fsh = psum_f.tile([P, width], F32, name="fsh")
+            for b in range(width // P):
+                block = slice(inner + b * P, inner + (b + 1) * P)
+                terms = (rest[half, t], plus[half, t], plus[half, t])
+                for j, term in enumerate(terms):
+                    nc.tensor.matmul(
+                        fsh[:, b * P : (b + 1) * P], term[:, block], ident[:],
+                        start=(j == 0), stop=(j == len(terms) - 1), is_transpose=True,
+                    )
+            state[step] = {"bt": bt, "bm": bm, "fsh": fsh}
+
+        def lobe(step):
+            c0, width, t = step
+            half, inner = divmod(c0, BANK)
+            lobe_sb = ring2.tile([P, width], F32, name="lobe_sb")
+            nc.vector.tensor_tensor(
+                lobe_sb[:], rough_win[t][:].indirect(mat_sb[:, c0 // 16 : (c0 + width) // 16]),
+                lh_sq[half, t][:, inner : inner + width], ALU.mult,
+            )
+            state[step]["lobe"] = lobe_sb
+
+        def pair_tile(step, label):
+            c0, width, t = step
+            key = (label, c0, t // 2)
+            if key not in state:
+                state[key] = ring2.tile([P, 2, width], F32, name=label)
+            return state[key]
+
+        def sheen(step):
+            c0, width, t = step
+            sheen_sb = ring2.tile([P, width], F32, name="sheen_sb")
+            nc.vector.tensor_tensor(sheen_sb[:], state[step]["fsh"][:], state[step]["bt"][:], ALU.mult)
+            nc.scalar.activation(pair_tile(step, "gate")[:, t % 2, :], sheen_sb[:], ACT.Sigmoid)
+
+        def rim(step):
+            c0, width, t = step
+            rim_sb = ring2.tile([P, width], F32, name="rim_sb")
+            nc.vector.scalar_tensor_tensor(
+                rim_sb[:], state[step]["lobe"][:], coef[:, 2, t : t + 1], state[step]["fsh"][:], ALU.add, ALU.mult
+            )
+            state[step]["rim"] = rim_sb
+
+        def diffuse(step):
+            c0, width, t = step
+            nc.vector.scalar_tensor_tensor(
+                pair_tile(step, "diff")[:, t % 2, :], state[step]["rim"][:], coef[:, 3, t : t + 1],
+                state[step]["bm"][:], ALU.add, ALU.mult,
+            )
+
+        def hidden_pair(step):
+            c0, width, t = step
+            key = ("pairs", c0)
+            if key not in state:
+                state[key] = ring2.tile([P, 2, 2 * width], BF16, name="pairs", align_bytes=64)
+            nc.vector.scalar_tensor_tensor(
+                state[key][:, t // 2, :].rearrange("p (r e) -> p r e", e=2),
+                pair_tile(step, "gate")[:].rearrange("p e r -> p r e"),
+                -1.0 / 0.6,
+                pair_tile(step, "diff")[:].rearrange("p e r -> p r e"),
+                ALU.add, ALU.mult,
+            )
+
+        def weave(step):
+            c0, width, t = step
+            hid = ring2.tile([P, PACK * width], BF16, name="hid", align_bytes=64)
+            nc.vector.tensor_copy(
+                hid[:].bitcast(I32).rearrange("p (r g) -> p r g", g=2),
+                state["pairs", c0][:].bitcast(I32).rearrange("p g r -> p r g"),
+            )
+            state["hid", c0] = hid
+
+        def last_product(step):
+            c0, width, t = step
+            codes = ring2.tile([P, width], U32, name="codes", align_bytes=64)
+            plane = ring2.tile([P, width], U8, name="plane", align_bytes=64)
+            nc.vector.quantize_mx(out=codes[:].bitcast(FP8X4), scales=plane[:], in_=state["hid", c0][:])
+            for m in range(N // P):
+                acc = psum_mm.tile([P, width], F32, name="acc")
+                nc.tensor.matmul_mx(
+                    out=acc[:],
+                    lhsT=w3_sb[:, 2 * P * m : 2 * P * (m + 1)].bitcast(FP4X4),
+                    lhsT_scale=w3_plane[:, P * m : P * (m + 1)],
+                    rhs=codes[:].bitcast(FP8X4),
+                    rhs_scale=plane[:],
+                    start=True,
+                    stop=True,
+                )
+                result = ring3.tile([P, width], F32, name="result")
+                nc.scalar.copy(result[:], acc[:])
+                nc.sync.dma_start(out=out[P * m : P * (m + 1), c0 : c0 + width], in_=result[:])
+
+        for index in range(len(steps) + 2):
+            now = steps[index] if index < len(steps) else None
+            before = steps[index - 1] if 1 <= index <= len(steps) else None
+            older = steps[index - 2] if index >= 2 else None
+            if now is not None:
+                if index < PACK:
+                    rough_window(index)
+                    colour_window(index)
+                fetch(now)
+                lobe(now)
+            if older is not None and older[2] == PACK - 1:
+                last_product(older)
+            if before is not None:
+                diffuse(before)
+            if now is not None:
+                sheen(now)
+            if before is not None and before[2] % 2 == 1:
+                hidden_pair(before)
+            if now is not None:
+                rim(now)
+            if before is not None and before[2] == PACK - 1:
+                weave(before)

@@ -19,7 +19,9 @@ K, T, S, N, H, U = 512, 2048, 512, 256, 512, 1024
 PACK = 4
 BANK = 512
 WINDOW = S + 32
-CHUNKS = (512, 256, 256)
+CHUNKS = (256, 256, 256, 128, 128)
+PRODUCT_BANKS = (0, 1, 2, 3)
+SUM_BANKS = (4, 5, 6, 7)
 FLOPS = 2 * (2 * K * H * S + H * N * U)
 
 
@@ -36,9 +38,8 @@ def tile_picked_ydisny_weak_p_kernel(
         keep = ctx.enter_context(tc.tile_pool(name="keep", bufs=1))
         ring2 = ctx.enter_context(tc.tile_pool(name="ring2", bufs=2))
         ring3 = ctx.enter_context(tc.tile_pool(name="ring3", bufs=3))
-        psum_t = ctx.enter_context(tc.psum_pool(name="psum_t", bufs=3))
-        psum_f = ctx.enter_context(tc.psum_pool(name="psum_f", bufs=3))
-        psum_mm = ctx.enter_context(tc.psum_pool(name="psum_mm", bufs=2))
+        psum = ctx.enter_context(tc.psum_pool(name="psum", bufs=1))
+        banks = [psum.tile([P, BANK], F32, name="bank%d" % b) for b in range(8)]
 
         offs_sb = keep.tile([P, S // 16], U16, name="offs_sb")
         mat_sb = keep.tile([P, U // 16], U16, name="mat_sb")
@@ -54,10 +55,11 @@ def tile_picked_ydisny_weak_p_kernel(
         bc_win = [keep.tile([P, WINDOW], F32, name="bc_win%d" % t) for t in range(PACK)]
         rough_win = [keep.tile([P, WINDOW], F32, name="rough_win%d" % t) for t in range(PACK)]
 
+        nc.gpsimd.memset(x_plane[:].bitcast(I32), 0)
         make_identity(nc, ident[:])
-        nc.vector.memset(x_plane[:].bitcast(I32), 0)
-        for plane in w_plane_raw + [w3_plane]:
-            nc.vector.memset(plane[:].bitcast(I32), 0)
+        for plane in w_plane_raw:
+            nc.gpsimd.memset(plane[:].bitcast(I32), 0)
+        nc.vector.memset(w3_plane[:].bitcast(I32), 0)
         for win in bc_win + rough_win:
             nc.vector.memset(win[:, S:WINDOW], 0.0)
 
@@ -65,45 +67,45 @@ def tile_picked_ydisny_weak_p_kernel(
         lh_rows = lh.rearrange("(p t) r -> p t r", t=PACK)
         nl_sb, lh_sb = {}, {}
 
-        def load_rows(held, rows, label, half, t0, t1):
-            piece = keep.tile([P, t1 - t0, BANK], F32, name="%s_%d_%d" % (label, half, t0))
-            nc.sync.dma_start(out=piece[:], in_=rows[:, t0:t1, half * BANK : (half + 1) * BANK])
-            for t in range(t0, t1):
-                held[half, t] = piece[:, t - t0, :]
+        def load_rows(held, rows, label, t, half0, half1):
+            piece = keep.tile([P, (half1 - half0) * BANK], F32, name="%s_%d_%d" % (label, t, half0))
+            nc.sync.dma_start(out=piece[:], in_=rows[:, t, half0 * BANK : half1 * BANK])
+            for half in range(half0, half1):
+                held[half, t] = piece[:, (half - half0) * BANK : (half - half0 + 1) * BANK]
 
         def load_words(tile, words):
             nc.sync.dma_start(out=tile[:].bitcast(I32), in_=words.bitcast(I32))
 
         load_rows(nl_sb, nl_rows, "nl", 0, 0, 1)
-        load_words(w_raw[0], w1_words[0])
-        load_words(w_raw[1], w2_words[0])
-        load_rows(nl_sb, nl_rows, "nl", 0, 1, 2)
-        load_rows(nl_sb, nl_rows, "nl", 0, 2, 4)
-        load_scale_rows(nc.sync, w_plane_raw[0], w1_scales[0])
-        load_rows(lh_sb, lh_rows, "lh", 0, 0, 2)
-        load_scale_rows(nc.sync, w_plane_raw[1], w2_scales[0])
-        load_rows(nl_sb, nl_rows, "nl", 1, 0, 2)
         nc.sync.dma_start(offs_sb[:], offs)
         load_scale_rows(nc.sync, x_plane, x_scales[0])
-        load_rows(lh_sb, lh_rows, "lh", 0, 2, 4)
-        load_rows(nl_sb, nl_rows, "nl", 1, 2, 4)
-        nc.sync.dma_start(out=x_table[:], in_=x_words[0].rearrange("p c j -> p (c j)").bitcast(I32))
-        load_rows(lh_sb, lh_rows, "lh", 1, 0, 2)
+        load_rows(nl_sb, nl_rows, "nl", 0, 1, 2)
+        load_rows(nl_sb, nl_rows, "nl", 1, 0, 2)
         nc.sync.dma_start(out=unit_sb[:], in_=unit.rearrange("(p t) o -> p (t o)", t=PACK))
+        load_scale_rows(nc.gpsimd, w_plane_raw[1], w2_scales[0])
+        load_words(w_raw[1], w2_words[0])
+        load_words(w_raw[0], w1_words[0])
+        load_rows(nl_sb, nl_rows, "nl", 2, 0, 2)
+        nc.sync.dma_start(out=x_table[:], in_=x_words[0].rearrange("p c j -> p (c j)").bitcast(I32))
+        load_rows(nl_sb, nl_rows, "nl", 3, 0, 2)
+        load_scale_rows(nc.sync, w_plane_raw[0], w1_scales[0])
+        load_rows(lh_sb, lh_rows, "lh", 0, 0, 2)
         nc.sync.dma_start(tint_sb[:], tint)
         nc.sync.dma_start(mat_sb[:], mat)
-        load_rows(lh_sb, lh_rows, "lh", 1, 2, 4)
+        load_rows(lh_sb, lh_rows, "lh", 1, 0, 2)
+        load_rows(lh_sb, lh_rows, "lh", 2, 0, 2)
+        load_rows(lh_sb, lh_rows, "lh", 3, 0, 2)
         load_words(w3_sb, w3_words[0])
         load_scale_rows(nc.sync, w3_plane, w3_scales[0])
 
         coef = keep.tile([P, 4, PACK], F32, name="coef")
         for row, factor in enumerate((-0.6 * 1.4, -0.6 * 0.4, 0.6 * 0.5, -0.6)):
-            nc.vector.tensor_scalar(coef[:, row, :], unit_sb[:], factor, 0.0, ALU.mult, ALU.add)
+            nc.gpsimd.tensor_scalar(coef[:, row, :], unit_sb[:], factor, 0.0, ALU.mult, ALU.add)
 
         plus, rest, lh_sq = {}, {}, {}
 
         def fsh_terms(half, t):
-            nl_t = psum_t.tile([P, BANK], F32, name="turned")
+            nl_t = banks[2 * t + half]
             for b in range(BANK // P):
                 nc.tensor.transpose(nl_t[:, b * P : (b + 1) * P], nl_sb[half, t][:, b * P : (b + 1) * P], ident[:])
             root = ring2.tile([P, BANK], F32, name="root")
@@ -116,7 +118,7 @@ def tile_picked_ydisny_weak_p_kernel(
             nc.vector.scalar_tensor_tensor(rest[half, t][:], nl_t[:], -2.3, inv[:], ALU.add, ALU.subtract)
 
         def square_lh(half, t):
-            lh_sq[half, t] = keep.tile([P, BANK], F32, name="lh_sq_%d_%d" % (half, t))
+            lh_sq[half, t] = keep.tile([P, BANK], F32, name="lh_sq", bufs=4)
             if (half, t) in ():
                 nc.scalar.activation(lh_sq[half, t][:], lh_sb[half, t], ACT.Square)
             else:
@@ -128,7 +130,7 @@ def tile_picked_ydisny_weak_p_kernel(
         w_plane = [keep.tile([P, PACK, P], U8, name="w_plane%d" % i, align_bytes=64) for i in range(2)]
 
         def deal_words(i):
-            nc.vector.tensor_copy(
+            nc.gpsimd.tensor_copy(
                 w_dealt[i][:].rearrange("p t (m e) -> p t m e", e=2),
                 w_raw[i][:].rearrange("p (m t e) -> p t m e", t=PACK, e=2),
             )
@@ -136,8 +138,8 @@ def tile_picked_ydisny_weak_p_kernel(
         def deal_scales(i):
             nc.gpsimd.tensor_copy(w_plane[i][:], w_plane_raw[i][:].rearrange("p (m t) -> p t m", t=PACK))
 
-        def first_product(i, t, pool, label):
-            acc = pool.tile([P, S], F32, name=label)
+        def first_product(i, t):
+            acc = banks[PRODUCT_BANKS[(2 * t + 1 - i) % len(PRODUCT_BANKS)]]
             nc.tensor.matmul_mx(
                 out=acc[:],
                 lhsT=w_dealt[i][:, t, :].bitcast(FP4X4),
@@ -150,35 +152,34 @@ def tile_picked_ydisny_weak_p_kernel(
             return acc
 
         def colour_window(t):
-            acc = first_product(0, t, psum_mm, "acc")
+            acc = first_product(0, t)
             nc.scalar.copy(bc_win[t][:, :S], acc[:])
 
         def rough_window(t):
-            acc = first_product(1, t, psum_t, "turned")
+            acc = first_product(1, t)
             sig = ring2.tile([P, S], F32, name="sig")
             nc.scalar.activation(sig[:], acc[:], ACT.Sigmoid)
             nc.vector.tensor_scalar(
                 rough_win[t][:, :S], sig[:], coef[:, 0, t : t + 1], coef[:, 1, t : t + 1], ALU.mult, ALU.add
             )
 
-        units = [(half, t) for half in range(U // BANK) for t in range(PACK)]
-        deal_words(0)
+        units = [(half, t) for t in range(PACK) for half in range(U // BANK)]
+        nc.vector.tensor_copy(xq_plane[:], x_plane[:].indirect(offs_sb[:]))
         deal_words(1)
+        deal_words(0)
+        deal_scales(1)
+        deal_scales(0)
         for index, (half, t) in enumerate(units):
             fsh_terms(half, t)
-            square_lh(half, t)
-            if index == 1:
-                deal_scales(0)
-                deal_scales(1)
-            if index == 4:
-                nc.vector.tensor_copy(xq_plane[:], x_plane[:].indirect(offs_sb[:]))
-            if index == 6:
+            if index < 4:
+                square_lh(half, t)
+            if index == 3:
                 nc.vector.tensor_copy(xq_words[:], x_table[:].bitcast(U32).indirect(offs_sb[:]))
 
-        steps = []
+        steps = [(half * BANK, BANK, t) for half, t in units[: -(U // BANK)]]
         start = 0
         for width in CHUNKS:
-            steps.extend([(start, width, t) for t in range(PACK)])
+            steps.append((start, width, PACK - 1))
             start = start + width
         state = {}
 
@@ -190,7 +191,7 @@ def tile_picked_ydisny_weak_p_kernel(
             nc.scalar.activation(bt[:], bc_win[t][:].indirect(tint_sb[:, lists]), ACT.Copy)
             bm = ring3.tile([P, width], F32, name="bm")
             nc.scalar.activation(bm[:], bc_win[t][:].indirect(mat_sb[:, lists]), ACT.Copy)
-            fsh = psum_f.tile([P, width], F32, name="fsh")
+            fsh = banks[SUM_BANKS[steps.index(step) % len(SUM_BANKS)]][:, :width]
             for b in range(width // P):
                 block = slice(inner + b * P, inner + (b + 1) * P)
                 terms = (rest[half, t], plus[half, t], plus[half, t])
@@ -213,10 +214,11 @@ def tile_picked_ydisny_weak_p_kernel(
 
         def pair_tile(step, label):
             c0, width, t = step
-            key = (label, c0, t // 2)
+            half, inner = divmod(c0, BANK)
+            key = (label, half, t // 2)
             if key not in state:
-                state[key] = ring2.tile([P, 2, width], F32, name=label)
-            return state[key]
+                state[key] = ring3.tile([P, 2, BANK], F32, name=label)
+            return state[key][:, :, inner : inner + width]
 
         def sheen(step):
             c0, width, t = step
@@ -241,23 +243,26 @@ def tile_picked_ydisny_weak_p_kernel(
 
         def hidden_pair(step):
             c0, width, t = step
-            key = ("pairs", c0)
+            half, inner = divmod(c0, BANK)
+            key = ("pairs", half)
             if key not in state:
-                state[key] = ring2.tile([P, 2, 2 * width], BF16, name="pairs", align_bytes=64)
+                state[key] = ring2.tile([P, 2, 2 * BANK], BF16, name="pairs", align_bytes=64)
             nc.vector.scalar_tensor_tensor(
-                state[key][:, t // 2, :].rearrange("p (r e) -> p r e", e=2),
-                pair_tile(step, "gate")[:].rearrange("p e r -> p r e"),
+                state[key][:, t // 2, 2 * inner : 2 * (inner + width)].rearrange("p (r e) -> p r e", e=2),
+                pair_tile(step, "gate").rearrange("p e r -> p r e"),
                 -1.0 / 0.6,
-                pair_tile(step, "diff")[:].rearrange("p e r -> p r e"),
+                pair_tile(step, "diff").rearrange("p e r -> p r e"),
                 ALU.add, ALU.mult,
             )
 
         def weave(step):
             c0, width, t = step
+            half, inner = divmod(c0, BANK)
             hid = ring2.tile([P, PACK * width], BF16, name="hid", align_bytes=64)
-            nc.vector.tensor_copy(
-                hid[:].bitcast(I32).rearrange("p (r g) -> p r g", g=2),
-                state["pairs", c0][:].bitcast(I32).rearrange("p g r -> p r g"),
+            move, word = (nc.vector.tensor_copy, I32) if c0 + width == U else (nc.scalar.copy, U32)
+            move(
+                hid[:].bitcast(word).rearrange("p (r g) -> p r g", g=2),
+                state["pairs", half][:].bitcast(word)[:, :, inner : inner + width].rearrange("p g r -> p r g"),
             )
             state["hid", c0] = hid
 
@@ -267,7 +272,7 @@ def tile_picked_ydisny_weak_p_kernel(
             plane = ring2.tile([P, width], U8, name="plane", align_bytes=64)
             nc.vector.quantize_mx(out=codes[:].bitcast(FP8X4), scales=plane[:], in_=state["hid", c0][:])
             for m in range(N // P):
-                acc = psum_mm.tile([P, width], F32, name="acc")
+                acc = banks[PRODUCT_BANKS[(2 * (steps.index(step) % 2) + m) % len(PRODUCT_BANKS)]][:, :width]
                 nc.tensor.matmul_mx(
                     out=acc[:],
                     lhsT=w3_sb[:, 2 * P * m : 2 * P * (m + 1)].bitcast(FP4X4),
@@ -277,8 +282,11 @@ def tile_picked_ydisny_weak_p_kernel(
                     start=True,
                     stop=True,
                 )
-                result = ring3.tile([P, width], F32, name="result")
-                nc.scalar.copy(result[:], acc[:])
+                result = keep.tile([P, width], F32, name="result_%d_%d" % (c0, m))
+                if m == 0 and c0 + width == U:
+                    nc.vector.tensor_copy(result[:], acc[:])
+                else:
+                    nc.scalar.copy(result[:], acc[:])
                 nc.sync.dma_start(out=out[P * m : P * (m + 1), c0 : c0 + width], in_=result[:])
 
         for index in range(len(steps) + 2):
@@ -286,20 +294,20 @@ def tile_picked_ydisny_weak_p_kernel(
             before = steps[index - 1] if 1 <= index <= len(steps) else None
             older = steps[index - 2] if index >= 2 else None
             if now is not None:
-                if index < PACK:
-                    rough_window(index)
-                    colour_window(index)
+                if now[0] == 0:
+                    rough_window(now[2])
+                    colour_window(now[2])
                 fetch(now)
                 lobe(now)
+                if index + 4 < len(units):
+                    square_lh(*units[index + 4])
+                sheen(now)
+                rim(now)
             if older is not None and older[2] == PACK - 1:
                 last_product(older)
             if before is not None:
                 diffuse(before)
-            if now is not None:
-                sheen(now)
-            if before is not None and before[2] % 2 == 1:
-                hidden_pair(before)
-            if now is not None:
-                rim(now)
-            if before is not None and before[2] == PACK - 1:
-                weave(before)
+                if before[2] % 2 == 1:
+                    hidden_pair(before)
+                if before[2] == PACK - 1:
+                    weave(before)

@@ -18,16 +18,19 @@ P = 128
 K, T, S, N, H, U = 512, 2048, 512, 256, 512, 1024
 PACK = 4
 BANK = 512
+HALVES = U // BANK
 WINDOW = S + 32
-CHUNKS = (256, 256, 256, 128, 128)
-PRODUCT_BANKS = (0, 1, 2, 3)
-SUM_BANKS = (4, 5, 6, 7)
+LAST_WIDTHS = (256, 256, 256, 128, 128)
+SQUARES_AHEAD = 4
+PRODUCT_BANKS = (0, 1, 2, 3, 4, 5, 2, 3)
+SUM_BANKS = (6, 7, 0, 1)
+RESULT_BANKS = (4, 5, 2, 3)
 FLOPS = 2 * (2 * K * H * S + H * N * U)
 
 
-def load_scale_rows(queue, plane, rows):
+def load_scale_rows(nc, plane, rows):
     for q in range(4):
-        queue.dma_start(out=plane[32 * q : 32 * q + 4, :].bitcast(I32), in_=rows[4 * q : 4 * q + 4, :].bitcast(I32))
+        nc.sync.dma_start(out=plane[32 * q : 32 * q + 4, :].bitcast(I32), in_=rows[4 * q : 4 * q + 4, :].bitcast(I32))
 
 
 def tile_picked_ydisny_weak_p_kernel(
@@ -52,7 +55,7 @@ def tile_picked_ydisny_weak_p_kernel(
         w3_plane = keep.tile([P, N], U8, name="w3_plane", align_bytes=64)
         unit_sb = keep.tile([P, PACK], F32, name="unit_sb")
         ident = keep.tile([P, P], F32, name="ident")
-        bc_win = [keep.tile([P, WINDOW], F32, name="bc_win%d" % t) for t in range(PACK)]
+        colour_win = [keep.tile([P, WINDOW], F32, name="colour_win%d" % t) for t in range(PACK)]
         rough_win = [keep.tile([P, WINDOW], F32, name="rough_win%d" % t) for t in range(PACK)]
 
         nc.gpsimd.memset(x_plane[:].bitcast(I32), 0)
@@ -60,7 +63,7 @@ def tile_picked_ydisny_weak_p_kernel(
         for plane in w_plane_raw:
             nc.gpsimd.memset(plane[:].bitcast(I32), 0)
         nc.vector.memset(w3_plane[:].bitcast(I32), 0)
-        for win in bc_win + rough_win:
+        for win in colour_win + rough_win:
             nc.vector.memset(win[:, S:WINDOW], 0.0)
 
         nl_rows = nl.rearrange("(p t) r -> p t r", t=PACK)
@@ -78,68 +81,66 @@ def tile_picked_ydisny_weak_p_kernel(
 
         load_rows(nl_sb, nl_rows, "nl", 0, 0, 1)
         nc.sync.dma_start(offs_sb[:], offs)
-        load_scale_rows(nc.sync, x_plane, x_scales[0])
+        load_scale_rows(nc, x_plane, x_scales[0])
         load_rows(nl_sb, nl_rows, "nl", 0, 1, 2)
         load_rows(nl_sb, nl_rows, "nl", 1, 0, 2)
         nc.sync.dma_start(out=unit_sb[:], in_=unit.rearrange("(p t) o -> p (t o)", t=PACK))
-        load_scale_rows(nc.gpsimd, w_plane_raw[1], w2_scales[0])
         load_words(w_raw[1], w2_words[0])
         load_words(w_raw[0], w1_words[0])
         load_rows(nl_sb, nl_rows, "nl", 2, 0, 2)
-        nc.sync.dma_start(out=x_table[:], in_=x_words[0].rearrange("p c j -> p (c j)").bitcast(I32))
+        load_scale_rows(nc, w_plane_raw[1], w2_scales[0])
         load_rows(nl_sb, nl_rows, "nl", 3, 0, 2)
-        load_scale_rows(nc.sync, w_plane_raw[0], w1_scales[0])
+        nc.sync.dma_start(out=x_table[:], in_=x_words[0].rearrange("p c j -> p (c j)").bitcast(I32))
         load_rows(lh_sb, lh_rows, "lh", 0, 0, 2)
+        load_scale_rows(nc, w_plane_raw[0], w1_scales[0])
         nc.sync.dma_start(tint_sb[:], tint)
         nc.sync.dma_start(mat_sb[:], mat)
         load_rows(lh_sb, lh_rows, "lh", 1, 0, 2)
         load_rows(lh_sb, lh_rows, "lh", 2, 0, 2)
         load_rows(lh_sb, lh_rows, "lh", 3, 0, 2)
         load_words(w3_sb, w3_words[0])
-        load_scale_rows(nc.sync, w3_plane, w3_scales[0])
+        load_scale_rows(nc, w3_plane, w3_scales[0])
 
         coef = keep.tile([P, 4, PACK], F32, name="coef")
         for row, factor in enumerate((-0.6 * 1.4, -0.6 * 0.4, 0.6 * 0.5, -0.6)):
             nc.gpsimd.tensor_scalar(coef[:, row, :], unit_sb[:], factor, 0.0, ALU.mult, ALU.add)
 
-        plus, rest, lh_sq = {}, {}, {}
+        plus, rest, lh_sq, fsh_sb = {}, {}, {}, {}
 
         def fsh_terms(half, t):
-            nl_t = banks[2 * t + half]
-            for b in range(BANK // P):
-                nc.tensor.transpose(nl_t[:, b * P : (b + 1) * P], nl_sb[half, t][:, b * P : (b + 1) * P], ident[:])
-            root = ring2.tile([P, BANK], F32, name="root")
-            nc.scalar.activation(root[:], nl_t[:], ACT.Abs_reciprocal_sqrt, bias=0.3 / 1.69, scale=1.0 / 1.69)
-            inv = ring3.tile([P, BANK], F32, name="inv")
-            nc.scalar.activation(inv[:], root[:], ACT.Square)
+            if t < 0:
+                cosine = nl_sb[half, t]
+            else:
+                cosine = banks[HALVES * (t - 0) + half][:]
+                for b in range(BANK // P):
+                    nc.tensor.transpose(cosine[:, b * P : (b + 1) * P], nl_sb[half, t][:, b * P : (b + 1) * P], ident[:])
+            root = keep.tile([P, BANK], F32, name="root", bufs=4)
+            nc.scalar.activation(root[:], cosine, ACT.Abs_reciprocal_sqrt, bias=0.3 / 1.69, scale=1.0 / 1.69)
+            inv = keep.tile([P, BANK], F32, name="inv", bufs=4)
+            if 1 <= HALVES * t + half <= 3:
+                nc.gpsimd.tensor_tensor(inv[:], root[:], root[:], ALU.mult)
+            else:
+                nc.scalar.activation(inv[:], root[:], ACT.Square)
             plus[half, t] = keep.tile([P, BANK], F32, name="plus_%d_%d" % (half, t))
             rest[half, t] = keep.tile([P, BANK], F32, name="rest_%d_%d" % (half, t))
-            nc.vector.scalar_tensor_tensor(plus[half, t][:], nl_t[:], -0.3, inv[:], ALU.is_gt, ALU.mult)
-            nc.vector.scalar_tensor_tensor(rest[half, t][:], nl_t[:], -2.3, inv[:], ALU.add, ALU.subtract)
+            nc.vector.scalar_tensor_tensor(plus[half, t][:], cosine, -0.3, inv[:], ALU.is_gt, ALU.mult)
+            nc.vector.scalar_tensor_tensor(rest[half, t][:], cosine, -2.3, inv[:], ALU.add, ALU.subtract)
+
+        def fsh_direct(half, t):
+            fsh_sb[half, t] = keep.tile([P, BANK], F32, name="fsh_%d_%d" % (half, t))
+            nc.vector.scalar_tensor_tensor(fsh_sb[half, t][:], plus[half, t][:], 2.0, rest[half, t][:], ALU.mult, ALU.add)
 
         def square_lh(half, t):
-            lh_sq[half, t] = keep.tile([P, BANK], F32, name="lh_sq", bufs=4)
-            if (half, t) in ():
-                nc.scalar.activation(lh_sq[half, t][:], lh_sb[half, t], ACT.Square)
-            else:
-                nc.gpsimd.tensor_tensor(lh_sq[half, t][:], lh_sb[half, t], lh_sb[half, t], ALU.mult)
+            lh_sq[half, t] = keep.tile([P, BANK], F32, name="lh_sq", bufs=SQUARES_AHEAD)
+            nc.gpsimd.tensor_tensor(lh_sq[half, t][:], lh_sb[half, t], lh_sb[half, t], ALU.mult)
 
         xq_words = keep.tile([P, S], U32, name="xq_words", align_bytes=64)
         xq_plane = keep.tile([P, S], U8, name="xq_plane", align_bytes=64)
         w_dealt = [keep.tile([P, PACK, 2 * P], U8, name="w_dealt%d" % i, align_bytes=64) for i in range(2)]
         w_plane = [keep.tile([P, PACK, P], U8, name="w_plane%d" % i, align_bytes=64) for i in range(2)]
 
-        def deal_words(i):
-            nc.gpsimd.tensor_copy(
-                w_dealt[i][:].rearrange("p t (m e) -> p t m e", e=2),
-                w_raw[i][:].rearrange("p (m t e) -> p t m e", t=PACK, e=2),
-            )
-
-        def deal_scales(i):
-            nc.gpsimd.tensor_copy(w_plane[i][:], w_plane_raw[i][:].rearrange("p (m t) -> p t m", t=PACK))
-
         def first_product(i, t):
-            acc = banks[PRODUCT_BANKS[(2 * t + 1 - i) % len(PRODUCT_BANKS)]]
+            acc = banks[PRODUCT_BANKS[2 * t + 1 - i]]
             nc.tensor.matmul_mx(
                 out=acc[:],
                 lhsT=w_dealt[i][:, t, :].bitcast(FP4X4),
@@ -151,56 +152,62 @@ def tile_picked_ydisny_weak_p_kernel(
             )
             return acc
 
-        def colour_window(t):
-            acc = first_product(0, t)
-            nc.scalar.copy(bc_win[t][:, :S], acc[:])
-
-        def rough_window(t):
-            acc = first_product(1, t)
+        def windows(t):
             sig = ring2.tile([P, S], F32, name="sig")
-            nc.scalar.activation(sig[:], acc[:], ACT.Sigmoid)
+            nc.scalar.activation(sig[:], first_product(1, t)[:], ACT.Sigmoid)
             nc.vector.tensor_scalar(
                 rough_win[t][:, :S], sig[:], coef[:, 0, t : t + 1], coef[:, 1, t : t + 1], ALU.mult, ALU.add
             )
+            nc.scalar.copy(colour_win[t][:, :S], first_product(0, t)[:])
 
-        units = [(half, t) for t in range(PACK) for half in range(U // BANK)]
+        units = [(half, t) for t in range(PACK) for half in range(HALVES)]
         nc.vector.tensor_copy(xq_plane[:], x_plane[:].indirect(offs_sb[:]))
-        deal_words(1)
-        deal_words(0)
-        deal_scales(1)
-        deal_scales(0)
+        for i in (1, 0):
+            nc.vector.tensor_copy(
+                w_dealt[i][:].rearrange("p t (m e) -> p t m e", e=2),
+                w_raw[i][:].rearrange("p (m t e) -> p t m e", t=PACK, e=2),
+            )
+        for i in (1, 0):
+            nc.gpsimd.tensor_copy(w_plane[i][:], w_plane_raw[i][:].rearrange("p (m t) -> p t m", t=PACK))
         for index, (half, t) in enumerate(units):
             fsh_terms(half, t)
-            if index < 4:
+            if 1 <= index <= HALVES * 0:
+                fsh_direct(*units[index - 1])
+            if index < SQUARES_AHEAD:
                 square_lh(half, t)
             if index == 3:
                 nc.vector.tensor_copy(xq_words[:], x_table[:].bitcast(U32).indirect(offs_sb[:]))
 
-        steps = [(half * BANK, BANK, t) for half, t in units[: -(U // BANK)]]
+        steps = [(half * BANK, BANK, t) for half, t in units[:-HALVES]]
         start = 0
-        for width in CHUNKS:
+        for width in LAST_WIDTHS:
             steps.append((start, width, PACK - 1))
             start = start + width
         state = {}
 
         def fetch(step):
             c0, width, t = step
-            lists = slice(c0 // 16, (c0 + width) // 16)
+            columns = slice(c0 // 16, (c0 + width) // 16)
             half, inner = divmod(c0, BANK)
-            bt = ring3.tile([P, width], F32, name="bt")
-            nc.scalar.activation(bt[:], bc_win[t][:].indirect(tint_sb[:, lists]), ACT.Copy)
-            bm = ring3.tile([P, width], F32, name="bm")
-            nc.scalar.activation(bm[:], bc_win[t][:].indirect(mat_sb[:, lists]), ACT.Copy)
-            fsh = banks[SUM_BANKS[steps.index(step) % len(SUM_BANKS)]][:, :width]
-            for b in range(width // P):
-                block = slice(inner + b * P, inner + (b + 1) * P)
-                terms = (rest[half, t], plus[half, t], plus[half, t])
-                for j, term in enumerate(terms):
-                    nc.tensor.matmul(
-                        fsh[:, b * P : (b + 1) * P], term[:, block], ident[:],
-                        start=(j == 0), stop=(j == len(terms) - 1), is_transpose=True,
-                    )
-            state[step] = {"bt": bt, "bm": bm, "fsh": fsh}
+            held = {}
+            if t >= 0:
+                held["bt"] = ring3.tile([P, width], F32, name="bt")
+                nc.scalar.activation(held["bt"][:], colour_win[t][:].indirect(tint_sb[:, columns]), ACT.Copy)
+            held["bm"] = ring3.tile([P, width], F32, name="bm")
+            nc.scalar.activation(held["bm"][:], colour_win[t][:].indirect(mat_sb[:, columns]), ACT.Copy)
+            if t < 0:
+                held["fsh"] = fsh_sb[half, t][:]
+            else:
+                held["fsh"] = banks[SUM_BANKS[steps.index(step) % len(SUM_BANKS)]][:, :width]
+                for b in range(width // P):
+                    block = slice(inner + b * P, inner + (b + 1) * P)
+                    terms = (rest[half, t], plus[half, t], plus[half, t])
+                    for j, term in enumerate(terms):
+                        nc.tensor.matmul(
+                            held["fsh"][:, b * P : (b + 1) * P], term[:, block], ident[:],
+                            start=(j == 0), stop=(j == len(terms) - 1), is_transpose=True,
+                        )
+            state[step] = held
 
         def lobe(step):
             c0, width, t = step
@@ -212,7 +219,7 @@ def tile_picked_ydisny_weak_p_kernel(
             )
             state[step]["lobe"] = lobe_sb
 
-        def pair_tile(step, label):
+        def pair_slice(step, label):
             c0, width, t = step
             half, inner = divmod(c0, BANK)
             key = (label, half, t // 2)
@@ -222,22 +229,25 @@ def tile_picked_ydisny_weak_p_kernel(
 
         def sheen(step):
             c0, width, t = step
-            sheen_sb = ring2.tile([P, width], F32, name="sheen_sb")
-            nc.vector.tensor_tensor(sheen_sb[:], state[step]["fsh"][:], state[step]["bt"][:], ALU.mult)
-            nc.scalar.activation(pair_tile(step, "gate")[:, t % 2, :], sheen_sb[:], ACT.Sigmoid)
+            both = pair_slice(step, "sheen")
+            nc.vector.tensor_tensor(both[:, t % 2, :], state[step]["fsh"], state[step]["bt"][:], ALU.mult)
+            if t % 2 == 1:
+                gate = ring2.tile([P, width, 2], F32, name="gate")
+                nc.scalar.activation(gate[:], both.rearrange("p e r -> p r e"), ACT.Sigmoid)
+                state[step]["gate"] = gate
 
         def rim(step):
             c0, width, t = step
             rim_sb = ring2.tile([P, width], F32, name="rim_sb")
             nc.vector.scalar_tensor_tensor(
-                rim_sb[:], state[step]["lobe"][:], coef[:, 2, t : t + 1], state[step]["fsh"][:], ALU.add, ALU.mult
+                rim_sb[:], state[step]["lobe"][:], coef[:, 2, t : t + 1], state[step]["fsh"], ALU.add, ALU.mult
             )
             state[step]["rim"] = rim_sb
 
         def diffuse(step):
             c0, width, t = step
             nc.vector.scalar_tensor_tensor(
-                pair_tile(step, "diff")[:, t % 2, :], state[step]["rim"][:], coef[:, 3, t : t + 1],
+                pair_slice(step, "diff")[:, t % 2, :], state[step]["rim"][:], coef[:, 3, t : t + 1],
                 state[step]["bm"][:], ALU.add, ALU.mult,
             )
 
@@ -249,9 +259,9 @@ def tile_picked_ydisny_weak_p_kernel(
                 state[key] = ring2.tile([P, 2, 2 * BANK], BF16, name="pairs", align_bytes=64)
             nc.vector.scalar_tensor_tensor(
                 state[key][:, t // 2, 2 * inner : 2 * (inner + width)].rearrange("p (r e) -> p r e", e=2),
-                pair_tile(step, "gate").rearrange("p e r -> p r e"),
+                state[step]["gate"][:],
                 -1.0 / 0.6,
-                pair_tile(step, "diff").rearrange("p e r -> p r e"),
+                pair_slice(step, "diff").rearrange("p e r -> p r e"),
                 ALU.add, ALU.mult,
             )
 
@@ -272,9 +282,9 @@ def tile_picked_ydisny_weak_p_kernel(
             plane = ring2.tile([P, width], U8, name="plane", align_bytes=64)
             nc.vector.quantize_mx(out=codes[:].bitcast(FP8X4), scales=plane[:], in_=state["hid", c0][:])
             for m in range(N // P):
-                acc = banks[PRODUCT_BANKS[(2 * (steps.index(step) % 2) + m) % len(PRODUCT_BANKS)]][:, :width]
+                acc = banks[RESULT_BANKS[(2 * steps.index(step) + m) % len(RESULT_BANKS)]][:, :width]
                 nc.tensor.matmul_mx(
-                    out=acc[:],
+                    out=acc,
                     lhsT=w3_sb[:, 2 * P * m : 2 * P * (m + 1)].bitcast(FP4X4),
                     lhsT_scale=w3_plane[:, P * m : P * (m + 1)],
                     rhs=codes[:].bitcast(FP8X4),
@@ -284,9 +294,9 @@ def tile_picked_ydisny_weak_p_kernel(
                 )
                 result = keep.tile([P, width], F32, name="result_%d_%d" % (c0, m))
                 if m == 0 and c0 + width == U:
-                    nc.vector.tensor_copy(result[:], acc[:])
+                    nc.vector.tensor_copy(result[:], acc)
                 else:
-                    nc.scalar.copy(result[:], acc[:])
+                    nc.scalar.copy(result[:], acc)
                 nc.sync.dma_start(out=out[P * m : P * (m + 1), c0 : c0 + width], in_=result[:])
 
         for index in range(len(steps) + 2):
@@ -295,12 +305,11 @@ def tile_picked_ydisny_weak_p_kernel(
             older = steps[index - 2] if index >= 2 else None
             if now is not None:
                 if now[0] == 0:
-                    rough_window(now[2])
-                    colour_window(now[2])
+                    windows(now[2])
                 fetch(now)
                 lobe(now)
-                if index + 4 < len(units):
-                    square_lh(*units[index + 4])
+                if index + SQUARES_AHEAD < len(units):
+                    square_lh(*units[index + SQUARES_AHEAD])
                 sheen(now)
                 rim(now)
             if older is not None and older[2] == PACK - 1:

@@ -83,16 +83,16 @@ def tile_picked_ydisny_weak_p_kernel(
         nc.sync.dma_start(offs_sb[:], offs)
         load_scale_rows(nc, x_plane, x_scales[0])
         load_rows(nl_sb, nl_rows, "nl", 0, 1, 2)
-        load_rows(nl_sb, nl_rows, "nl", 1, 0, 2)
-        nc.sync.dma_start(out=unit_sb[:], in_=unit.rearrange("(p t) o -> p (t o)", t=PACK))
         load_words(w_raw[1], w2_words[0])
         load_words(w_raw[0], w1_words[0])
+        nc.sync.dma_start(out=unit_sb[:], in_=unit.rearrange("(p t) o -> p (t o)", t=PACK))
+        load_rows(nl_sb, nl_rows, "nl", 1, 0, 2)
         load_rows(nl_sb, nl_rows, "nl", 2, 0, 2)
         load_scale_rows(nc, w_plane_raw[1], w2_scales[0])
         load_rows(nl_sb, nl_rows, "nl", 3, 0, 2)
         nc.sync.dma_start(out=x_table[:], in_=x_words[0].rearrange("p c j -> p (c j)").bitcast(I32))
-        load_rows(lh_sb, lh_rows, "lh", 0, 0, 2)
         load_scale_rows(nc, w_plane_raw[0], w1_scales[0])
+        load_rows(lh_sb, lh_rows, "lh", 0, 0, 2)
         nc.sync.dma_start(tint_sb[:], tint)
         nc.sync.dma_start(mat_sb[:], mat)
         load_rows(lh_sb, lh_rows, "lh", 1, 0, 2)
@@ -117,8 +117,10 @@ def tile_picked_ydisny_weak_p_kernel(
             root = keep.tile([P, BANK], F32, name="root", bufs=4)
             nc.scalar.activation(root[:], cosine, ACT.Abs_reciprocal_sqrt, bias=0.3 / 1.69, scale=1.0 / 1.69)
             inv = keep.tile([P, BANK], F32, name="inv", bufs=4)
-            if 1 <= HALVES * t + half <= 3:
+            if 2 <= HALVES * t + half <= 3:
                 nc.gpsimd.tensor_tensor(inv[:], root[:], root[:], ALU.mult)
+            elif HALVES * t + half == 0:
+                nc.vector.tensor_tensor(inv[:], root[:], root[:], ALU.mult)
             else:
                 nc.scalar.activation(inv[:], root[:], ACT.Square)
             plus[half, t] = keep.tile([P, BANK], F32, name="plus_%d_%d" % (half, t))
@@ -155,9 +157,14 @@ def tile_picked_ydisny_weak_p_kernel(
         def windows(t):
             sig = ring2.tile([P, S], F32, name="sig")
             nc.scalar.activation(sig[:], first_product(1, t)[:], ACT.Sigmoid)
-            nc.vector.tensor_scalar(
-                rough_win[t][:, :S], sig[:], coef[:, 0, t : t + 1], coef[:, 1, t : t + 1], ALU.mult, ALU.add
-            )
+            if t == 3:
+                nc.scalar.activation(
+                    rough_win[t][:, :S], sig[:], ACT.Identity, bias=coef[:, 1, t : t + 1], scale=coef[:, 0, t : t + 1]
+                )
+            else:
+                nc.vector.tensor_scalar(
+                    rough_win[t][:, :S], sig[:], coef[:, 0, t : t + 1], coef[:, 1, t : t + 1], ALU.mult, ALU.add
+                )
             nc.scalar.copy(colour_win[t][:, :S], first_product(0, t)[:])
 
         units = [(half, t) for t in range(PACK) for half in range(HALVES)]

from contextlib import ExitStack

import concourse.mybir as mybir
from concourse.masks import make_identity

F32 = mybir.dt.float32
BF16 = mybir.dt.bfloat16
I32 = mybir.dt.int32
U32 = mybir.dt.uint32
U16 = mybir.dt.uint16
U8 = mybir.dt.uint8
FP8X4 = mybir.dt.float8_e4m3fn_x4
FP4X4 = mybir.dt.float4_e2m1fn_x4
ACT = mybir.ActivationFunctionType
ALU = mybir.AluOpType

P = 128
K, T, S, N, H, U = 512, 2048, 512, 256, 512, 1024
PACK = 4
BANK = 512
HALVES = U // BANK
WINDOW = S + 32
LAST_WIDTHS = (256, 256, 256, 128, 128)
SQUARES_AHEAD = 4
PRODUCT_BANKS = (0, 1, 2, 3, 4, 5, 2, 3)
SUM_BANKS = (6, 7, 0, 1)
RESULT_BANKS = (4, 5, 2, 3)
FLOPS = 2 * (2 * K * H * S + H * N * U)


def load_scale_rows(nc, plane, rows):
    for q in range(4):
        nc.sync.dma_start(out=plane[32 * q : 32 * q + 4, :].bitcast(I32), in_=rows[4 * q : 4 * q + 4, :].bitcast(I32))


def tile_picked_ydisny_weak_p_kernel(
    tc, x_words, x_scales, w1_words, w1_scales, w2_words, w2_scales, nl, lh, unit, w3_words, w3_scales, offs, mat, tint, out
):
    nc = tc.nc
    with ExitStack() as ctx:
        keep = ctx.enter_context(tc.tile_pool(name="keep", bufs=1))
        ring2 = ctx.enter_context(tc.tile_pool(name="ring2", bufs=2))
        ring3 = ctx.enter_context(tc.tile_pool(name="ring3", bufs=3))
        psum = ctx.enter_context(tc.psum_pool(name="psum", bufs=1))
        banks = [psum.tile([P, BANK], F32, name="bank%d" % b) for b in range(8)]

        offs_sb = keep.tile([P, S // 16], U16, name="offs_sb")
        mat_sb = keep.tile([P, U // 16], U16, name="mat_sb")
        tint_sb = keep.tile([P, U // 16], U16, name="tint_sb")
        x_table = keep.tile([P, T], I32, name="x_table", align_bytes=64)
        x_plane = keep.tile([P, T], U8, name="x_plane", align_bytes=64)
        w_raw = [keep.tile([P, 2 * H], U8, name="w_raw%d" % i, align_bytes=64) for i in range(2)]
        w_plane_raw = [keep.tile([P, H], U8, name="w_plane_raw%d" % i, align_bytes=64) for i in range(2)]
        w3_sb = keep.tile([P, 2 * N], U8, name="w3_sb", align_bytes=64)
        w3_plane = keep.tile([P, N], U8, name="w3_plane", align_bytes=64)
        unit_sb = keep.tile([P, PACK], F32, name="unit_sb")
        ident = keep.tile([P, P], F32, name="ident")
        colour_win = [keep.tile([P, WINDOW], F32, name="colour_win%d" % t) for t in range(PACK)]
        rough_win = [keep.tile([P, WINDOW], F32, name="rough_win%d" % t) for t in range(PACK)]

        nc.gpsimd.memset(x_plane[:].bitcast(I32), 0)
        make_identity(nc, ident[:])
        for plane in w_plane_raw:
            nc.gpsimd.memset(plane[:].bitcast(I32), 0)
        nc.vector.memset(w3_plane[:].bitcast(I32), 0)
        for win in colour_win + rough_win:
            nc.vector.memset(win[:, S:WINDOW], 0.0)

        nl_rows = nl.rearrange("(p t) r -> p t r", t=PACK)
        lh_rows = lh.rearrange("(p t) r -> p t r", t=PACK)
        nl_sb, lh_sb = {}, {}

        def load_rows(held, rows, label, t, half0, half1):
            piece = keep.tile([P, (half1 - half0) * BANK], F32, name="%s_%d_%d" % (label, t, half0))
            nc.sync.dma_start(out=piece[:], in_=rows[:, t, half0 * BANK : half1 * BANK])
            for half in range(half0, half1):
                held[half, t] = piece[:, (half - half0) * BANK : (half - half0 + 1) * BANK]

        def load_words(tile, words):
            nc.sync.dma_start(out=tile[:].bitcast(I32), in_=words.bitcast(I32))

        load_rows(nl_sb, nl_rows, "nl", 0, 0, 1)
        nc.sync.dma_start(offs_sb[:], offs)
        load_scale_rows(nc, x_plane, x_scales[0])
        load_rows(nl_sb, nl_rows, "nl", 0, 1, 2)
        load_words(w_raw[1], w2_words[0])
        load_words(w_raw[0], w1_words[0])
        nc.sync.dma_start(out=unit_sb[:], in_=unit.rearrange("(p t) o -> p (t o)", t=PACK))
        load_rows(nl_sb, nl_rows, "nl", 1, 0, 2)
        load_rows(nl_sb, nl_rows, "nl", 2, 0, 2)
        load_scale_rows(nc, w_plane_raw[1], w2_scales[0])
        load_rows(nl_sb, nl_rows, "nl", 3, 0, 2)
        nc.sync.dma_start(out=x_table[:], in_=x_words[0].rearrange("p c j -> p (c j)").bitcast(I32))
        load_scale_rows(nc, w_plane_raw[0], w1_scales[0])
        load_rows(lh_sb, lh_rows, "lh", 0, 0, 2)
        nc.sync.dma_start(tint_sb[:], tint)
        nc.sync.dma_start(mat_sb[:], mat)
        load_rows(lh_sb, lh_rows, "lh", 1, 0, 2)
        load_rows(lh_sb, lh_rows, "lh", 2, 0, 2)
        load_rows(lh_sb, lh_rows, "lh", 3, 0, 2)
        load_words(w3_sb, w3_words[0])
        load_scale_rows(nc, w3_plane, w3_scales[0])

        coef = keep.tile([P, 4, PACK], F32, name="coef")
        for row, factor in enumerate((-0.6 * 1.4, -0.6 * 0.4, 0.6 * 0.5, -0.6)):
            nc.gpsimd.tensor_scalar(coef[:, row, :], unit_sb[:], factor, 0.0, ALU.mult, ALU.add)

        plus, rest, lh_sq, fsh_sb = {}, {}, {}, {}

        def fsh_terms(half, t):
            if t < 0:
                cosine = nl_sb[half, t]
            else:
                cosine = banks[HALVES * (t - 0) + half][:]
                for b in range(BANK // P):
                    nc.tensor.transpose(cosine[:, b * P : (b + 1) * P], nl_sb[half, t][:, b * P : (b + 1) * P], ident[:])
            root = keep.tile([P, BANK], F32, name="root", bufs=4)
            nc.scalar.activation(root[:], cosine, ACT.Abs_reciprocal_sqrt, bias=0.3 / 1.69, scale=1.0 / 1.69)
            inv = keep.tile([P, BANK], F32, name="inv", bufs=4)
            if 2 <= HALVES * t + half <= 3:
                nc.gpsimd.tensor_tensor(inv[:], root[:], root[:], ALU.mult)
            elif HALVES * t + half == 0:
                nc.vector.tensor_tensor(inv[:], root[:], root[:], ALU.mult)
            else:
                nc.scalar.activation(inv[:], root[:], ACT.Square)
            plus[half, t] = keep.tile([P, BANK], F32, name="plus_%d_%d" % (half, t))
            rest[half, t] = keep.tile([P, BANK], F32, name="rest_%d_%d" % (half, t))
            nc.vector.scalar_tensor_tensor(plus[half, t][:], cosine, -0.3, inv[:], ALU.is_gt, ALU.mult)
            nc.vector.scalar_tensor_tensor(rest[half, t][:], cosine, -2.3, inv[:], ALU.add, ALU.subtract)

        def fsh_direct(half, t):
            fsh_sb[half, t] = keep.tile([P, BANK], F32, name="fsh_%d_%d" % (half, t))
            nc.vector.scalar_tensor_tensor(fsh_sb[half, t][:], plus[half, t][:], 2.0, rest[half, t][:], ALU.mult, ALU.add)

        def square_lh(half, t):
            lh_sq[half, t] = keep.tile([P, BANK], F32, name="lh_sq", bufs=SQUARES_AHEAD)
            nc.gpsimd.tensor_tensor(lh_sq[half, t][:], lh_sb[half, t], lh_sb[half, t], ALU.mult)

        xq_words = keep.tile([P, S], U32, name="xq_words", align_bytes=64)
        xq_plane = keep.tile([P, S], U8, name="xq_plane", align_bytes=64)
        w_dealt = [keep.tile([P, PACK, 2 * P], U8, name="w_dealt%d" % i, align_bytes=64) for i in range(2)]
        w_plane = [keep.tile([P, PACK, P], U8, name="w_plane%d" % i, align_bytes=64) for i in range(2)]

        def first_product(i, t):
            acc = banks[PRODUCT_BANKS[2 * t + 1 - i]]
            nc.tensor.matmul_mx(
                out=acc[:],
                lhsT=w_dealt[i][:, t, :].bitcast(FP4X4),
                lhsT_scale=w_plane[i][:, t, :],
                rhs=xq_words[:].bitcast(FP8X4),
                rhs_scale=xq_plane[:],
                start=True,
                stop=True,
            )
            return acc

        def windows(t):
            sig = ring2.tile([P, S], F32, name="sig")
            nc.scalar.activation(sig[:], first_product(1, t)[:], ACT.Sigmoid)
            if t == 3:
                nc.scalar.activation(
                    rough_win[t][:, :S], sig[:], ACT.Identity, bias=coef[:, 1, t : t + 1], scale=coef[:, 0, t : t + 1]
                )
            else:
                nc.vector.tensor_scalar(
                    rough_win[t][:, :S], sig[:], coef[:, 0, t : t + 1], coef[:, 1, t : t + 1], ALU.mult, ALU.add
                )
            nc.scalar.copy(colour_win[t][:, :S], first_product(0, t)[:])

        units = [(half, t) for t in range(PACK) for half in range(HALVES)]
        nc.vector.tensor_copy(xq_plane[:], x_plane[:].indirect(offs_sb[:]))
        for i in (1, 0):
            nc.vector.tensor_copy(
                w_dealt[i][:].rearrange("p t (m e) -> p t m e", e=2),
                w_raw[i][:].rearrange("p (m t e) -> p t m e", t=PACK, e=2),
            )
        for i in (1, 0):
            nc.gpsimd.tensor_copy(w_plane[i][:], w_plane_raw[i][:].rearrange("p (m t) -> p t m", t=PACK))
        for index, (half, t) in enumerate(units):
            fsh_terms(half, t)
            if 1 <= index <= HALVES * 0:
                fsh_direct(*units[index - 1])
            if index < SQUARES_AHEAD:
                square_lh(half, t)
            if index == 3:
                nc.vector.tensor_copy(xq_words[:], x_table[:].bitcast(U32).indirect(offs_sb[:]))

        steps = [(half * BANK, BANK, t) for half, t in units[:-HALVES]]
        start = 0
        for width in LAST_WIDTHS:
            steps.append((start, width, PACK - 1))
            start = start + width
        state = {}

        def fetch(step):
            c0, width, t = step
            columns = slice(c0 // 16, (c0 + width) // 16)
            half, inner = divmod(c0, BANK)
            held = {}
            if t >= 0:
                held["bt"] = ring3.tile([P, width], F32, name="bt")
                nc.scalar.activation(held["bt"][:], colour_win[t][:].indirect(tint_sb[:, columns]), ACT.Copy)
            held["bm"] = ring3.tile([P, width], F32, name="bm")
            nc.scalar.activation(held["bm"][:], colour_win[t][:].indirect(mat_sb[:, columns]), ACT.Copy)
            if t < 0:
                held["fsh"] = fsh_sb[half, t][:]
            else:
                held["fsh"] = banks[SUM_BANKS[steps.index(step) % len(SUM_BANKS)]][:, :width]
                for b in range(width // P):
                    block = slice(inner + b * P, inner + (b + 1) * P)
                    terms = (rest[half, t], plus[half, t], plus[half, t])
                    for j, term in enumerate(terms):
                        nc.tensor.matmul(
                            held["fsh"][:, b * P : (b + 1) * P], term[:, block], ident[:],
                            start=(j == 0), stop=(j == len(terms) - 1), is_transpose=True,
                        )
            state[step] = held

        def lobe(step):
            c0, width, t = step
            half, inner = divmod(c0, BANK)
            lobe_sb = ring2.tile([P, width], F32, name="lobe_sb")
            nc.vector.tensor_tensor(
                lobe_sb[:], rough_win[t][:].indirect(mat_sb[:, c0 // 16 : (c0 + width) // 16]),
                lh_sq[half, t][:, inner : inner + width], ALU.mult,
            )
            state[step]["lobe"] = lobe_sb

        def pair_slice(step, label):
            c0, width, t = step
            half, inner = divmod(c0, BANK)
            key = (label, half, t // 2)
            if key not in state:
                state[key] = ring3.tile([P, 2, BANK], F32, name=label)
            return state[key][:, :, inner : inner + width]

        def sheen(step):
            c0, width, t = step
            both = pair_slice(step, "sheen")
            nc.vector.tensor_tensor(both[:, t % 2, :], state[step]["fsh"], state[step]["bt"][:], ALU.mult)
            if t % 2 == 1:
                gate = ring2.tile([P, width, 2], F32, name="gate")
                nc.scalar.activation(gate[:], both.rearrange("p e r -> p r e"), ACT.Sigmoid)
                state[step]["gate"] = gate

        def rim(step):
            c0, width, t = step
            rim_sb = ring2.tile([P, width], F32, name="rim_sb")
            nc.vector.scalar_tensor_tensor(
                rim_sb[:], state[step]["lobe"][:], coef[:, 2, t : t + 1], state[step]["fsh"], ALU.add, ALU.mult
            )
            state[step]["rim"] = rim_sb

        def diffuse(step):
            c0, width, t = step
            nc.vector.scalar_tensor_tensor(
                pair_slice(step, "diff")[:, t % 2, :], state[step]["rim"][:], coef[:, 3, t : t + 1],
                state[step]["bm"][:], ALU.add, ALU.mult,
            )

        def hidden_pair(step):
            c0, width, t = step
            half, inner = divmod(c0, BANK)
            key = ("pairs", half)
            if key not in state:
                state[key] = ring2.tile([P, 2, 2 * BANK], BF16, name="pairs", align_bytes=64)
            nc.vector.scalar_tensor_tensor(
                state[key][:, t // 2, 2 * inner : 2 * (inner + width)].rearrange("p (r e) -> p r e", e=2),
                state[step]["gate"][:],
                -1.0 / 0.6,
                pair_slice(step, "diff").rearrange("p e r -> p r e"),
                ALU.add, ALU.mult,
            )

        def weave(step):
            c0, width, t = step
            half, inner = divmod(c0, BANK)
            hid = ring2.tile([P, PACK * width], BF16, name="hid", align_bytes=64)
            move, word = (nc.vector.tensor_copy, I32) if c0 + width == U else (nc.scalar.copy, U32)
            move(
                hid[:].bitcast(word).rearrange("p (r g) -> p r g", g=2),
                state["pairs", half][:].bitcast(word)[:, :, inner : inner + width].rearrange("p g r -> p r g"),
            )
            state["hid", c0] = hid

        def last_product(step):
            c0, width, t = step
            codes = ring2.tile([P, width], U32, name="codes", align_bytes=64)
            plane = ring2.tile([P, width], U8, name="plane", align_bytes=64)
            nc.vector.quantize_mx(out=codes[:].bitcast(FP8X4), scales=plane[:], in_=state["hid", c0][:])
            for m in range(N // P):
                acc = banks[RESULT_BANKS[(2 * steps.index(step) + m) % len(RESULT_BANKS)]][:, :width]
                nc.tensor.matmul_mx(
                    out=acc,
                    lhsT=w3_sb[:, 2 * P * m : 2 * P * (m + 1)].bitcast(FP4X4),
                    lhsT_scale=w3_plane[:, P * m : P * (m + 1)],
                    rhs=codes[:].bitcast(FP8X4),
                    rhs_scale=plane[:],
                    start=True,
                    stop=True,
                )
                result = keep.tile([P, width], F32, name="result_%d_%d" % (c0, m))
                if m == 0 and c0 + width == U:
                    nc.vector.tensor_copy(result[:], acc)
                else:
                    nc.scalar.copy(result[:], acc)
                nc.sync.dma_start(out=out[P * m : P * (m + 1), c0 : c0 + width], in_=result[:])

        for index in range(len(steps) + 2):
            now = steps[index] if index < len(steps) else None
            before = steps[index - 1] if 1 <= index <= len(steps) else None
            older = steps[index - 2] if index >= 2 else None
            if now is not None:
                if now[0] == 0:
                    windows(now[2])
                fetch(now)
                lobe(now)
                if index + SQUARES_AHEAD < len(units):
                    square_lh(*units[index + SQUARES_AHEAD])
                sheen(now)
                rim(now)
            if older is not None and older[2] == PACK - 1:
                last_product(older)
            if before is not None:
                diffuse(before)
                if before[2] % 2 == 1:
                    hidden_pair(before)
                if before[2] == PACK - 1:
                    weave(before)
